import numpy as np, ml_dtypes
CORES = [10,34,74,98]
N = 4
import mx_ref
BF = ml_dtypes.bfloat16
def entries(a):
    return np.ascontiguousarray(a.T).reshape(-1)
def table(e):
    return np.ascontiguousarray(np.reshape(e, (-1, 16)).T).astype(np.int32)
def cols(t, e):
    v = np.concatenate([t.reshape(128, -1, 4), np.zeros((128, 1, 4), BF)], axis=1)
    return np.ascontiguousarray(v[:, e]).reshape(128, -1)
def f(rng, *shape):
    return mx_ref.flush((rng.standard_normal(shape, dtype=np.float32) * np.exp2(rng.integers(-2, 3, shape[:-1] + (1,)))).astype(BF))
def wide(rng, *shape, cols=0):
    v = rng.standard_normal(shape, dtype=np.float32) * np.exp2(rng.integers(-12, 13, shape)).astype(np.float32)
    if cols: v *= np.repeat(np.exp2(rng.integers(-cols, cols + 1, shape[:-2] + (1, shape[-1] // 4))) * (rng.random(shape[:-2] + (1, shape[-1] // 4)) > 0.0625), 4, axis=-1).astype(np.float32)
    return mx_ref.flush(v.astype(BF))
T, S, CAPP = 1024, 256, 96
def lists(rng, most=None, own=False, share=False, edge=False):
    o, c, m = [], [], []
    for r in range(N):
        n = np.zeros(N, int)
        if own: n[r] = CAPP
        if most is not None:
            for q in rng.permutation(N)[:most]: n[q] = CAPP
            n = np.minimum(n, np.maximum(0, S - (np.cumsum(n) - n)))
        while n.sum() < S:
            q = rng.integers(0, N)
            if n[q] < CAPP: n[q] += 1
        slots = np.full(N * CAPP, -1); used = []
        for q in range(N):
            k = q * CAPP + rng.permutation(CAPP)[:n[q]]; used += list(k)
            slots[k] = rng.integers(0, T) if share else rng.choice([0, T - 1], n[q]) if edge else rng.integers(0, T, n[q])
        o.append(table(rng.choice([0, T - 1], S) if edge else rng.integers(0, T, S))); c.append(table(slots)); m.append(table(rng.permutation(used)))
    return {"own": np.stack(o), "want": np.stack(c), "slot": np.stack(m)}
def setup_inputs(rng):
    return {"x": f(rng, N, 128, 4 * T), "w": f(rng, N, 128, 512), **lists(rng)}
def setup_inputs_edge(rng):
    return {**setup_inputs(rng), **lists(rng, edge=True)}
def setup_inputs_full(rng):
    return {**setup_inputs(rng), **lists(rng, most=S // CAPP)}
def setup_inputs_self(rng):
    return {**setup_inputs(rng), **lists(rng, own=True)}
def setup_inputs_share(rng):
    return {**setup_inputs(rng), **lists(rng, share=True)}
def setup_inputs_spread(rng):
    d = setup_inputs(rng); d["x"] = wide(rng, N, 128, 4 * T, cols=8); return d
def check_inputs(d):
    b = []
    for r in range(N):
        o, c, m = entries(d["own"][r]), entries(d["want"][r]), entries(d["slot"][r])
        if o.min() < 0 or o.max() >= T: b.append("own")
        if c.min() < -1 or c.max() >= T: b.append("want")
        if m.min() < 0 or m.max() >= N * CAPP or len(set(m.tolist())) != S or (c[m] < 0).any() or (c >= 0).sum() != S: b.append("slot")
    return b
def decode(q):
    out = np.zeros(q[0].shape, np.float32)
    for b in range(4):
        e = np.zeros((128, 128, 4), np.float32); e[np.arange(128), np.arange(128), b] = 1
        out[:, b::4] = mx_ref.matmul(mx_ref.quantize(e.reshape(128, 512).astype(BF)), q)
    return out
def reference(x, w, own, want, slot):
    M = []
    for r in range(N):
        c = entries(want[r])
        arrived = np.concatenate([decode(mx_ref.quantize(cols(x[q], c[q * CAPP:(q + 1) * CAPP]))) for q in range(N)], axis=1)
        far = arrived.reshape(128, -1, 4)[:, entries(slot[r])].reshape(128, -1)
        M.append(mx_ref.quantize(((cols(x[r], entries(own[r])).astype(np.float32) + far) * np.float32(0.5)).astype(BF)))
    y = np.zeros((N, 128, 3 * S), np.float32)
    for r in range(N):
        for i in range(3): y[r][:, S * i:S * i + S] = mx_ref.matmul(mx_ref.quantize(w[r]), M[(r - 1 + i) % N])
    return {"y": y}

@@ -1,0 +1,278 @@
+from concourse.bass import DstId, RemoteDMATransfer
+from concourse.mybir import dt, AluOpType, ActivationFunctionType
+
+N, S, CAPP, R = 4, 256, 96, 1024
+POS = [0, 3, 1, 2]
+H = 2 * CAPP
+PAD = 128 - CAPP
+F8 = "float8_e4m3fn_x4"
+
+SCRATCH = {
+    "xs": ("sbuf", [128, 4 * R], "bfloat16"),
+    "ws": ("sbuf", [128, 512], "bfloat16"),
+    "wl": ("sbuf", [128, 24], "int32"), "sl": ("sbuf", [128, 16], "int32"), "ol": ("sbuf", [128, 512], "int32"),
+    "w16": ("sbuf", [128, 24], "uint16"),
+    "lopp": ("sbuf", [128, 6], "uint16"), "lpair": ("sbuf", [128, 12], "uint16"),
+    "u1": ("sbuf", [128, 16], "int32"), "u2": ("sbuf", [128, 16], "int32"), "u3": ("sbuf", [128, 16], "int32"),
+    "pos": ("sbuf", [128, 16], "int32"), "hi": ("sbuf", [128, 16], "int32"),
+    "pos16": ("sbuf", [128, 16], "uint16"), "pprev": ("sbuf", [128, 16], "uint16"), "pnext": ("sbuf", [128, 16], "uint16"),
+    "so": ("sbuf", [128, 32], "float32"), "sot": ("sbuf", [128, 32], "float32"), "so16": ("sbuf", [128, 32], "uint16"),
+    "flat": ("sbuf", [128, 768], "float32"), "flatt": ("sbuf", [128, 768], "float32"), "own16": ("sbuf", [128, 24], "uint16"),
+    "half": ("sbuf", [128, 128], "bfloat16"), "ident": ("sbuf", [128, 128], "bfloat16"),
+    "et": ("sbuf", [128, 2048], "bfloat16"), "ec": ("sbuf", [128, 512], F8), "ep": ("sbuf", [128, 512], "uint8"),
+    "wc": ("sbuf", [128, 128], F8), "wp": ("sbuf", [128, 128], "uint8"),
+    "topp": ("sbuf", [128, 512], "bfloat16"), "tself": ("sbuf", [128, 512], "bfloat16"), "tpair": ("sbuf", [128, 4 * H], "bfloat16"),
+    "oppc": ("sbuf", [128, 128], F8), "oppp": ("sbuf", [128, 128], "uint8"),
+    "pairc": ("sbuf", [128, H], F8), "pairp": ("sbuf", [128, H], "uint8"),
+    "lac": ("sbuf", [128, H + PAD], F8), "lap": ("sbuf", [128, H + PAD], "uint8"),
+    "lbc": ("sbuf", [128, H], F8), "lbp": ("sbuf", [128, H], "uint8"),
+    "xa": ("sbuf", [128, 4 * H], "bfloat16"), "xb": ("sbuf", [128, 4 * H], "bfloat16"),
+    "ma": ("sbuf", [128, 4 * H], "bfloat16"), "mb": ("sbuf", [128, 4 * H], "bfloat16"),
+    "mc": ("sbuf", [128, 2 * H], F8), "mp": ("sbuf", [128, 2 * H], "uint8"),
+    "prevc": ("sbuf", [128, 2 * H], F8), "prevp": ("sbuf", [128, 2 * H], "uint8"),
+    "nextc": ("sbuf", [128, 2 * H], F8), "nextp": ("sbuf", [128, 2 * H], "uint8"),
+    "yw0": ("sbuf", [128, 2 * H], "float32"), "yw1": ("sbuf", [128, 2 * H], "float32"), "yw2": ("sbuf", [128, 2 * H], "float32"),
+    "ys0": ("sbuf", [128, S], "float32"), "ys1": ("sbuf", [128, S], "float32"), "ys2": ("sbuf", [128, S], "float32"),
+}
+for _k in range(8):
+    SCRATCH["ps%d" % _k] = ("psum", [128, 512], "float32")
+ARR = ["sent", "l_opp", "l_next", "l_prev", "p_next", "p_prev", "f_opp", "f_next", "f_prev",
+       "m_next0", "m_next1", "m_prev0", "m_prev1"]
+SEMAPHORES = ARR + ["e%d" % _k for _k in range(110)]
+
+
+def rank_program(g, core, T, topo):
+    r = T.rank_of(core)
+    if r is None:
+        return
+    V, A, PE, SY = g.vector, g.scalar, g.tensor, g.sync
+    queues = {"g": g, "V": V, "A": A, "PE": PE, "SY": SY}
+    add, mult = AluOpType.add, AluOpType.mult
+    COPY = ActivationFunctionType.Copy
+    nxt, prv, opp = (r + 1) % N, (r - 1) % N, (r + 2) % N
+    nevents = [0]
+    seen = set()
+    unwaited = {}
+
+    def event(n=1):
+        name = "e%d" % nevents[0]
+        nevents[0] += 1
+        unwaited[name] = n
+        return (name, n)
+
+    def wait(q, *evs):
+        for name, n in evs:
+            if (q, name) not in seen:
+                seen.add((q, name))
+                unwaited.pop(name, None)
+                queues[q].wait_ge(T.sem[name], n)
+
+    def done(ins, n=1):
+        e = event(n)
+        ins.then_inc(T.sem[e[0]], n)
+        return e
+
+    ha = POS[r] // 2
+    hb = 1 - ha
+
+    def a_base(k):
+        return PAD if POS[k] % 2 == 0 else 0
+
+    def a_col(k, q):
+        return a_base(k) + CAPP * (POS[q] % 2)
+
+    sent = [0]
+
+    def engs(k):
+        return topo.engines(core, T.cores[k])
+
+    def send(k, out, src, sem):
+        rid, pid, _ = topo.addr(T.cores[k])
+        g.remote_dma(out_ap=out, in_ap=src, remote_sem=T.sem[sem], local_sem=T.sem.sent, pid=pid, routing_id=rid,
+                     dma_engine_mask=topo.mask(core, T.cores[k]))
+        sent[0] += len(engs(k))
+
+    def send_two(items):
+        tr = []
+        for i, (k, out, src, sem) in enumerate(items):
+            es = engs(k)
+            es = es[i * len(es) // 2:(i + 1) * len(es) // 2]
+            sent[0] += len(es)
+            rid, pid, _ = topo.addr(T.cores[k])
+            tr.append(RemoteDMATransfer(dst_ids=[DstId(rid=rid, pnc=pid)], dma_engine_mask=sum(1 << e for e in es),
+                                        remote_sem=T.sem[sem], srcs=[src], dsts=[out]))
+        g.remote_dma_fused(tr, local_sem=T.sem.sent)
+
+    ne = len(engs(opp))
+
+    def u8(v):
+        return v.bitcast(dt.uint8)
+
+    e_want, e_slot, e_own, e_x, e_w, e_y = event(128), event(128), event(128), event(16), event(16), event(48)
+
+    def load(q, out, src, e):
+        q.dma_start(out, src).then_inc(T.sem[e[0]], 16)
+
+    for k in range(4):
+        load(SY, T.wl[16 * k:16 * k + 16, :], T.want[:], e_want)
+        load(A, T.wl[16 * k + 64:16 * k + 80, :], T.want[:], e_want)
+    load(SY, T.xs[:], T.x[:], e_x)
+    for k in range(8):
+        load(A, T.sl[16 * k:16 * k + 16, :], T.slot[:], e_slot)
+
+    v_half = done(V.memset(T.half[:], 0.5))
+    v_ol = done(V.memset(T.ol[:], 0))
+    v_et = done(V.memset(T.et[:], 0.0))
+    v_p1 = done(V.memset(T.topp[:, 4 * CAPP:512], 0.0))
+    s0 = 4 * PAD if a_base(r) else 0
+    v_p2 = done(V.memset(T.tself[:, 0:4 * PAD] if s0 else T.tself[:, 4 * CAPP:512], 0.0))
+    wait("A", v_ol)
+    for k in range(4):
+        for j in range(2):
+            load(A, T.ol[32 * k:32 * k + 1, 256 * j:256 * j + 256], T.own[:], e_own)
+    load(A, T.ws[:], T.w[:], e_w)
+    wait("g", v_half)
+    g_id = done(g.affine_select(T.ident[:], T.half[:], [[-1, 128]], AluOpType.is_equal, 0.0, 0, 1))
+    wait("A", v_et)
+    a_flat = done(A.activation(T.flat[:], T.et[:, 0:768], COPY))
+    wait("A", g_id, a_flat)
+    a_e = [done(A.activation(T.et[:, 512 * b + b:512 * b + 512:4], T.ident[:], COPY)) for b in range(4)]
+
+    wait("V", e_want)
+    v_w16 = done(V.tensor_scalar(T.w16[:], T.wl[:], 0, 4, AluOpType.max, mult))
+    wait("g", v_w16)
+
+    def wcols(k):
+        return T.w16[:, 6 * k:6 * k + 6]
+
+    send(opp, T.lopp[:], wcols(opp), "l_opp")
+    send_two([(nxt, T.lpair[:, 6:12], wcols(nxt), "l_prev"), (prv, T.lpair[:, 0:6], wcols(prv), "l_next")])
+
+    wait("V", e_slot)
+    v1 = done(V.tensor_scalar(T.u1[:], T.sl[:], CAPP, 2 * CAPP, AluOpType.is_ge, mult))
+    v2 = done(V.tensor_scalar(T.u2[:], T.sl[:], 2 * CAPP, -3 * CAPP, AluOpType.is_ge, mult))
+    wait("V", v1, v2)
+    v3 = done(V.tensor_tensor(T.u3[:], T.u1[:], T.u2[:], add))
+    wait("V", v3)
+    v_pos = done(V.tensor_tensor(T.pos[:], T.sl[:], T.u3[:], add))
+    wait("V", v_pos)
+    v_p16 = done(V.tensor_copy(T.pos16[:], T.pos[:]))
+    v_hi = done(V.tensor_scalar(T.hi[:], T.pos[:], 0x1F0, None, AluOpType.bitwise_and))
+    wait("g", v_p16)
+    send_two([(nxt, T.pprev[:], T.pos16[:], "p_prev"), (prv, T.pnext[:], T.pos16[:], "p_next")])
+    wait("V", v_hi)
+    v_s = [done(V.tensor_tensor(T.so[:, 16 * j:16 * j + 16], T.pos[:], T.hi[:], add)) for j in range(2)]
+    wait("V", *v_s)
+    v_t = done(V.transpose(T.sot[:], T.so[:]))
+    wait("V", v_t)
+    v_o = [done(V.tensor_copy(T.so16[:, 0:16], T.sot[:, 0:16])),
+           done(V.tensor_scalar(T.so16[:, 16:32], T.sot[:, 0:16], 16, None, add))]
+    wait("V", e_own, a_flat, *v_o)
+    v_sc = done(V.tensor_copy(T.flat[:, 0:768].indirect(T.so16[:, 0:32]), T.ol[:]))
+    wait("V", v_sc)
+    v_ft = done(V.transpose(T.flatt[:], T.flat[:]))
+    wait("V", v_ft)
+    v_own = done(V.tensor_scalar(T.own16[:], T.flatt[:, 0:768:32], 4, None, mult))
+
+    def xwin(t):
+        return T.xs[:, t:4 * R]
+
+    def gather(tile, a, n, off):
+        ev = []
+        for t in range(4):
+            out, src = tile[:, a + t:a + 4 * n:4], xwin(t).indirect(off)
+            ev.append(done(V.tensor_copy(out, src)) if t < 2 else done(A.activation(out, src, COPY)))
+        return ev
+
+    for q in ("V", "A"):
+        wait(q, e_x, ("l_opp", ne))
+    ev = gather(T.topp, 0, CAPP, T.lopp[:])
+    wait("V", v_p1, *ev)
+    v_qo = done(V.quantize_mx(T.oppc[:], T.oppp[:], T.topp[:]))
+    for q in ("V", "A"):
+        wait(q, ("l_next", ne // 2), ("l_prev", ne // 2))
+    ev = gather(T.tpair, 0, H, T.lpair[:])
+    wait("V", *ev)
+    v_qp = done(V.quantize_mx(T.pairc[:], T.pairp[:], T.tpair[:]))
+
+    wait("g", v_qo)
+    c = a_col(opp, r)
+    send(opp, u8(T.lac[:, c:c + CAPP]), u8(T.oppc[:, 0:CAPP]), "f_opp")
+    send(opp, T.lap[:, c:c + CAPP], T.oppp[:, 0:CAPP], "f_opp")
+    wait("g", v_qp)
+    c = CAPP * (POS[r] % 2)
+    send_two([(nxt, u8(T.lbc[:, c:c + CAPP]), u8(T.pairc[:, 0:CAPP]), "f_prev"),
+              (prv, u8(T.lbc[:, c:c + CAPP]), u8(T.pairc[:, CAPP:H]), "f_next")])
+    send_two([(nxt, T.lbp[:, c:c + CAPP], T.pairp[:, 0:CAPP], "f_prev"),
+              (prv, T.lbp[:, c:c + CAPP], T.pairp[:, CAPP:H], "f_next")])
+
+    wait("A", v_w16)
+    wait("V", v_w16)
+    ev = gather(T.tself, s0, CAPP, T.w16[:, 6 * r:6 * r + 6])
+    wait("V", v_p2, *ev)
+    c = a_col(r, r) - (PAD if s0 else 0)
+    v_qs = done(V.quantize_mx(T.lac[:, c:c + 128], T.lap[:, c:c + 128], T.tself[:]))
+    wait("V", *a_e)
+    v_qe = done(V.quantize_mx(T.ec[:], T.ep[:], T.et[:]))
+    wait("A", v_own)
+    wait("V", v_own)
+    ev_x = {}
+    for tile, h in ((T.xa, ha), (T.xb, hb)):
+        off = T.own16[:, 12 * h:12 * h + 12]
+        ev_x[h] = [done(V.tensor_scalar(tile[:, H * t:H * t + H], xwin(t).indirect(off), 0.5, None, mult)) if t < 2
+                   else done(A.activation(tile[:, H * t:H * t + H], xwin(t).indirect(off), COPY, scale=0.5))
+                   for t in range(4)]
+    wait("V", e_w)
+    v_qw = done(V.quantize_mx(T.wc[:], T.wp[:], T.ws[:]))
+
+    v_m, v_qm = {}, {}
+    for h, lc, lp, base, arr, xh, mt, bank in (
+            (ha, T.lac, T.lap, a_base(r), [v_qs, ("f_opp", 2 * ne)], T.xa, T.ma, 0),
+            (hb, T.lbc, T.lbp, 0, [("f_next", ne), ("f_prev", ne)], T.xb, T.mb, 4)):
+        wait("PE", v_qe, *arr)
+        dec = [done(PE.matmul_mx(T["ps%d" % (bank + b)][:, 0:H], T.ec[:, 128 * b:128 * b + 128], T.ep[:, 128 * b:128 * b + 128],
+                                 lc[:, base:base + H], lp[:, base:base + H], True, True)) for b in range(4)]
+        v_m[h] = []
+        for b in range(4):
+            wait("V", dec[b], ev_x[h][b])
+            v_m[h].append(done(V.tensor_tensor(mt[:, b:4 * H:4], T["ps%d" % (bank + b)][:, 0:H], xh[:, H * b:H * b + H], add)))
+        wait("V", *v_m[h])
+        v_qm[h] = done(V.quantize_mx(T.mc[:, H * h:H * h + H], T.mp[:, H * h:H * h + H], mt[:]))
+        wait("g", v_qm[h])
+        m = slice(H * h, H * h + H)
+        k = 0 if h == ha else 1
+        for src, on, op in ((u8(T.mc[:, m]), u8(T.prevc[:, m]), u8(T.nextc[:, m])), (T.mp[:, m], T.prevp[:, m], T.nextp[:, m])):
+            send_two([(nxt, on, src, "m_prev%d" % k), (prv, op, src, "m_next%d" % k)])
+
+    def product(bank, codes, plane, a, n):
+        return done(PE.matmul_mx(T["ps%d" % bank][:, 0:n], T.wc[:], T.wp[:], codes[:, a:a + n], plane[:, a:a + n], True, True))
+
+    wait("PE", v_qw, v_m[ha][2], v_qm[ha], v_qm[hb])
+    p_own = product(2, T.mc, T.mp, 0, 2 * H)
+    wait("A", p_own)
+    a_own = done(A.activation(T.yw1[:], T.ps2[:, 0:2 * H], COPY))
+    wait("A", a_own, v_p16)
+    a_y1 = done(A.activation(T.ys1[:], T.yw1[:].indirect(T.pos16[:]), COPY))
+    wait("SY", a_y1)
+    load(SY, T.y[:, S:2 * S], T.ys1[:], e_y)
+    cop = {"V": [], "A": []}
+    for k, h in ((0, hb), (1, ha)):
+        bank = 4 * k
+        for q, b, codes, plane, sem, win in (("V", bank, T.prevc, T.prevp, "m_prev%d" % k, T.yw0),
+                                             ("A", bank + 1, T.nextc, T.nextp, "m_next%d" % k, T.yw2)):
+            wait("PE", v_m[hb if k else ha][b % 4], (sem, ne))
+            p = product(b, codes, plane, H * h, H)
+            wait(q, p)
+            out, src = win[:, H * h:H * h + H], T["ps%d" % b][:, 0:H]
+            cop[q].append(done(V.tensor_copy(out, src) if q == "V" else A.activation(out, src, COPY)))
+    wait("V", ("p_prev", ne // 2), *cop["V"])
+    v_y0 = done(V.tensor_copy(T.ys0[:], T.yw0[:].indirect(T.pprev[:])))
+    wait("SY", v_y0)
+    load(SY, T.y[:, 0:S], T.ys0[:], e_y)
+    wait("A", ("p_next", ne // 2), *cop["A"])
+    a_y2 = done(A.activation(T.ys2[:], T.yw2[:].indirect(T.pnext[:]), COPY))
+    wait("A", a_y2)
+    load(A, T.y[:, 2 * S:3 * S], T.ys2[:], e_y)
+
+    wait("g", e_y, ("sent", sent[0]))
+    wait("g", *list(unwaited.items()))

@@ -6,39 +6,44 @@ POS = [0, 3, 1, 2]
 H = 2 * CAPP
 PAD = 128 - CAPP
 F8 = "float8_e4m3fn_x4"
+L_OPP, L_SELF, L_PREV, L_NEXT, L_ALL = 0, 128, 256, 352, 448
+M_A, M_B, M_ALL = PAD, H + 2 * PAD, 2 * H + 2 * PAD
+A_IN, B_IN, IN_ALL = 0, M_B - PAD, M_ALL - PAD
 
 SCRATCH = {
     "xs": ("sbuf", [128, 4 * R], "bfloat16"),
     "ws": ("sbuf", [128, 512], "bfloat16"),
-    "wl": ("sbuf", [128, 24], "int32"), "sl": ("sbuf", [128, 16], "int32"), "ol": ("sbuf", [128, 512], "int32"),
+    "wl": ("sbuf", [128, 24], "int32"), "sl": ("sbuf", [128, 16], "int32"), "ol": ("sbuf", [128, 256], "int32"),
     "w16": ("sbuf", [128, 24], "uint16"),
     "lopp": ("sbuf", [128, 6], "uint16"), "lpair": ("sbuf", [128, 12], "uint16"),
     "u1": ("sbuf", [128, 16], "int32"), "u2": ("sbuf", [128, 16], "int32"), "u3": ("sbuf", [128, 16], "int32"),
-    "pos": ("sbuf", [128, 16], "int32"), "hi": ("sbuf", [128, 16], "int32"),
+    "pos": ("sbuf", [128, 16], "int32"),
     "pos16": ("sbuf", [128, 16], "uint16"), "pprev": ("sbuf", [128, 16], "uint16"), "pnext": ("sbuf", [128, 16], "uint16"),
-    "so": ("sbuf", [128, 32], "float32"), "sot": ("sbuf", [128, 32], "float32"), "so16": ("sbuf", [128, 32], "uint16"),
-    "flat": ("sbuf", [128, 768], "float32"), "flatt": ("sbuf", [128, 768], "float32"), "own16": ("sbuf", [128, 24], "uint16"),
-    "half": ("sbuf", [128, 128], "bfloat16"), "ident": ("sbuf", [128, 128], "bfloat16"),
+    "so": ("sbuf", [128, 32], "float32"), "sot": ("sbuf", [128, 32], "float32"), "so16": ("sbuf", [128, 16], "uint16"),
+    "flat": ("sbuf", [128, 416], "float32"), "flatt": ("sbuf", [128, 416], "float32"),
+    "sel": ("sbuf", [128, 48], "float32"), "ownf": ("sbuf", [128, 24], "float32"), "own16": ("sbuf", [128, 24], "uint16"),
+    "pidx": ("sbuf", [128, 1], "int32"), "podd": ("sbuf", [128, 1], "int32"),
+    "odd16": ("sbuf", [128, 1], "float32"), "modd": ("sbuf", [128, 1], "float32"), "meven": ("sbuf", [128, 1], "float32"),
+    "half": ("sbuf", [128, 512], "bfloat16"), "ident": ("sbuf", [128, 128], "bfloat16"),
     "et": ("sbuf", [128, 2048], "bfloat16"), "ec": ("sbuf", [128, 512], F8), "ep": ("sbuf", [128, 512], "uint8"),
     "wc": ("sbuf", [128, 128], F8), "wp": ("sbuf", [128, 128], "uint8"),
-    "topp": ("sbuf", [128, 512], "bfloat16"), "tself": ("sbuf", [128, 512], "bfloat16"), "tpair": ("sbuf", [128, 4 * H], "bfloat16"),
+    "topp": ("sbuf", [128, 512], "bfloat16"), "tself": ("sbuf", [128, 640], "bfloat16"), "tpair": ("sbuf", [128, 4 * H], "bfloat16"),
     "oppc": ("sbuf", [128, 128], F8), "oppp": ("sbuf", [128, 128], "uint8"),
     "pairc": ("sbuf", [128, H], F8), "pairp": ("sbuf", [128, H], "uint8"),
-    "lac": ("sbuf", [128, H + PAD], F8), "lap": ("sbuf", [128, H + PAD], "uint8"),
-    "lbc": ("sbuf", [128, H], F8), "lbp": ("sbuf", [128, H], "uint8"),
-    "xa": ("sbuf", [128, 4 * H], "bfloat16"), "xb": ("sbuf", [128, 4 * H], "bfloat16"),
-    "ma": ("sbuf", [128, 4 * H], "bfloat16"), "mb": ("sbuf", [128, 4 * H], "bfloat16"),
-    "mc": ("sbuf", [128, 2 * H], F8), "mp": ("sbuf", [128, 2 * H], "uint8"),
-    "prevc": ("sbuf", [128, 2 * H], F8), "prevp": ("sbuf", [128, 2 * H], "uint8"),
-    "nextc": ("sbuf", [128, 2 * H], F8), "nextp": ("sbuf", [128, 2 * H], "uint8"),
+    "lc": ("sbuf", [128, L_ALL], F8), "lp": ("sbuf", [128, L_ALL], "uint8"),
+    "xh0": ("sbuf", [128, 4 * H], "bfloat16"), "xh1": ("sbuf", [128, 4 * H], "bfloat16"),
+    "ma": ("sbuf", [128, 4 * M_B], "bfloat16"), "mb": ("sbuf", [128, 4 * H], "bfloat16"),
+    "mc": ("sbuf", [128, M_ALL], F8), "mp": ("sbuf", [128, M_ALL], "uint8"),
+    "prevc": ("sbuf", [128, IN_ALL], F8), "prevp": ("sbuf", [128, IN_ALL], "uint8"),
+    "nextc": ("sbuf", [128, IN_ALL], F8), "nextp": ("sbuf", [128, IN_ALL], "uint8"),
     "yw0": ("sbuf", [128, 2 * H], "float32"), "yw1": ("sbuf", [128, 2 * H], "float32"), "yw2": ("sbuf", [128, 2 * H], "float32"),
     "ys0": ("sbuf", [128, S], "float32"), "ys1": ("sbuf", [128, S], "float32"), "ys2": ("sbuf", [128, S], "float32"),
 }
 for _k in range(8):
     SCRATCH["ps%d" % _k] = ("psum", [128, 512], "float32")
 ARR = ["sent", "l_opp", "l_next", "l_prev", "p_next", "p_prev", "f_opp", "f_next", "f_prev",
-       "m_next0", "m_next1", "m_prev0", "m_prev1"]
-SEMAPHORES = ARR + ["e%d" % _k for _k in range(110)]
+       "m_next0", "m_next1", "m_prev0", "m_prev1", "m_nextp", "m_prevp"]
+SEMAPHORES = ARR + ["e%d" % _k for _k in range(132)]
 
 
 def rank_program(g, core, T, topo):
@@ -75,12 +80,6 @@ def rank_program(g, core, T, topo):
     ha = POS[r] // 2
     hb = 1 - ha
 
-    def a_base(k):
-        return PAD if POS[k] % 2 == 0 else 0
-
-    def a_col(k, q):
-        return a_base(k) + CAPP * (POS[q] % 2)
-
     sent = [0]
 
     def engs(k):
@@ -104,11 +103,12 @@ def rank_program(g, core, T, topo):
         g.remote_dma_fused(tr, local_sem=T.sem.sent)
 
     ne = len(engs(opp))
+    nh = ne // 2
 
     def u8(v):
         return v.bitcast(dt.uint8)
 
-    e_want, e_slot, e_own, e_x, e_w, e_y = event(128), event(128), event(128), event(16), event(16), event(48)
+    e_want, e_slot, e_own, e_x, e_w, e_y = event(128), event(128), event(128), event(16), event(16), event(80)
 
     def load(q, out, src, e):
         q.dma_start(out, src).then_inc(T.sem[e[0]], 16)
@@ -120,23 +120,30 @@ def rank_program(g, core, T, topo):
     for k in range(8):
         load(A, T.sl[16 * k:16 * k + 16, :], T.slot[:], e_slot)
 
-    v_half = done(V.memset(T.half[:], 0.5))
+    g_p = done(g.iota(T.pidx[:], [[1, 1]], 0, 1))
     v_ol = done(V.memset(T.ol[:], 0))
-    v_et = done(V.memset(T.et[:], 0.0))
-    v_p1 = done(V.memset(T.topp[:, 4 * CAPP:512], 0.0))
-    s0 = 4 * PAD if a_base(r) else 0
-    v_p2 = done(V.memset(T.tself[:, 0:4 * PAD] if s0 else T.tself[:, 4 * CAPP:512], 0.0))
+    v_half = done(V.memset(T.half[:], 0.5))
+    v_pad = [done(V.memset(T.topp[:, 4 * CAPP:512], 0.0)), done(V.memset(T.tself[:, 0:4 * PAD], 0.0)),
+             done(V.memset(T.tself[:, 512:640], 0.0)), done(V.memset(T.ma[:, 0:4 * M_A], 0.0)),
+             done(V.memset(T.ma[:, 4 * (M_B - PAD):4 * M_B], 0.0))]
+    wait("V", g_p)
+    v_odd = done(V.tensor_scalar(T.podd[:], T.pidx[:], 16, None, AluOpType.bitwise_and))
+    wait("V", v_odd)
+    v_o16 = done(V.tensor_copy(T.odd16[:], T.podd[:]))
     wait("A", v_ol)
-    for k in range(4):
-        for j in range(2):
-            load(A, T.ol[32 * k:32 * k + 1, 256 * j:256 * j + 256], T.own[:], e_own)
+    for k in range(8):
+        load(A, T.ol[16 * k:16 * k + 1, :], T.own[:], e_own)
     load(A, T.ws[:], T.w[:], e_w)
     wait("g", v_half)
-    g_id = done(g.affine_select(T.ident[:], T.half[:], [[-1, 128]], AluOpType.is_equal, 0.0, 0, 1))
-    wait("A", v_et)
-    a_flat = done(A.activation(T.flat[:], T.et[:, 0:768], COPY))
-    wait("A", g_id, a_flat)
-    a_e = [done(A.activation(T.et[:, 512 * b + b:512 * b + 512:4], T.ident[:], COPY)) for b in range(4)]
+    g_id = done(g.affine_select(T.ident[:], T.half[:, 0:128], [[-1, 128]], AluOpType.is_equal, 0.0, 0, 1))
+    wait("A", v_half)
+    a_flat = done(A.activation(T.flat[:], T.half[:, 0:416], COPY, scale=0.0))
+    a_z = [done(A.activation(T.et[:, 512 * b:512 * b + 512], T.half[:], COPY, scale=0.0)) for b in range(4)]
+    wait("A", g_id)
+    a_e = []
+    for b in range(4):
+        wait("A", a_z[b])
+        a_e.append(done(A.activation(T.et[:, 512 * b + b:512 * b + 512:4], T.ident[:], COPY)))
 
     wait("V", e_want)
     v_w16 = done(V.tensor_scalar(T.w16[:], T.wl[:], 0, 4, AluOpType.max, mult))
@@ -154,25 +161,33 @@ def rank_program(g, core, T, topo):
     wait("V", v1, v2)
     v3 = done(V.tensor_tensor(T.u3[:], T.u1[:], T.u2[:], add))
     wait("V", v3)
+    v_s = [done(V.tensor_tensor(T.so[:, 16 * j:16 * j + 16], T.sl[:], T.u3[:], add)) for j in range(2)]
     v_pos = done(V.tensor_tensor(T.pos[:], T.sl[:], T.u3[:], add))
-    wait("V", v_pos)
-    v_p16 = done(V.tensor_copy(T.pos16[:], T.pos[:]))
-    v_hi = done(V.tensor_scalar(T.hi[:], T.pos[:], 0x1F0, None, AluOpType.bitwise_and))
-    wait("g", v_p16)
-    send_two([(nxt, T.pprev[:], T.pos16[:], "p_prev"), (prv, T.pnext[:], T.pos16[:], "p_next")])
-    wait("V", v_hi)
-    v_s = [done(V.tensor_tensor(T.so[:, 16 * j:16 * j + 16], T.pos[:], T.hi[:], add)) for j in range(2)]
     wait("V", *v_s)
     v_t = done(V.transpose(T.sot[:], T.so[:]))
-    wait("V", v_t)
-    v_o = [done(V.tensor_copy(T.so16[:, 0:16], T.sot[:, 0:16])),
-           done(V.tensor_scalar(T.so16[:, 16:32], T.sot[:, 0:16], 16, None, add))]
-    wait("V", e_own, a_flat, *v_o)
-    v_sc = done(V.tensor_copy(T.flat[:, 0:768].indirect(T.so16[:, 0:32]), T.ol[:]))
-    wait("V", v_sc)
+    wait("V", v_pos)
+    v_p16 = done(V.tensor_copy(T.pos16[:], T.pos[:]))
+    wait("g", v_p16)
+    send_two([(nxt, T.pprev[:], T.pos16[:], "p_prev"), (prv, T.pnext[:], T.pos16[:], "p_next")])
+    wait("V", v_t, v_o16)
+    v_o = done(V.tensor_scalar(T.so16[:], T.sot[:, 0:16], T.odd16[:], None, add))
+    v_mask = [done(V.tensor_scalar(T.modd[:], T.odd16[:], 0.25, None, mult)),
+              done(V.tensor_scalar(T.meven[:], T.odd16[:], -0.25, 4.0, mult, add))]
+    wait("V", e_own, a_flat, v_o)
+    v_sc = done(V.tensor_copy(T.flat[:].indirect(T.so16[:]), T.ol[:]))
+    wait("V", v_sc, *v_mask)
     v_ft = done(V.transpose(T.flatt[:], T.flat[:]))
     wait("V", v_ft)
-    v_own = done(V.tensor_scalar(T.own16[:], T.flatt[:, 0:768:32], 4, None, mult))
+    v_sel = [done(V.tensor_scalar(T.sel[:, 12 * j:12 * j + 12], T.flatt[:, a:e:32], m[:], None, mult))
+             for j, (a, e, m) in enumerate(((0, 384, T.meven), (16, 384, T.modd), (48, 416, T.meven), (0, 384, T.modd)))]
+    wait("V", *v_sel)
+    v_of = [done(V.tensor_tensor(T.ownf[:, j:24:2], T.sel[:, 24 * j:24 * j + 12], T.sel[:, 24 * j + 12:24 * j + 24], add)) for j in range(2)]
+    wait("V", *v_of)
+    v_own = done(V.tensor_copy(T.own16[:], T.ownf[:]))
+    wait("V", *a_e)
+    v_qe = done(V.quantize_mx(T.ec[:], T.ep[:], T.et[:]))
+    wait("V", e_w)
+    v_qw = done(V.quantize_mx(T.wc[:], T.wp[:], T.ws[:]))
 
     def xwin(t):
         return T.xs[:, t:4 * R]
@@ -187,92 +202,120 @@ def rank_program(g, core, T, topo):
     for q in ("V", "A"):
         wait(q, e_x, ("l_opp", ne))
     ev = gather(T.topp, 0, CAPP, T.lopp[:])
-    wait("V", v_p1, *ev)
+    wait("V", v_pad[0], *ev)
     v_qo = done(V.quantize_mx(T.oppc[:], T.oppp[:], T.topp[:]))
     for q in ("V", "A"):
-        wait(q, ("l_next", ne // 2), ("l_prev", ne // 2))
+        wait(q, ("l_next", nh), ("l_prev", nh))
     ev = gather(T.tpair, 0, H, T.lpair[:])
     wait("V", *ev)
     v_qp = done(V.quantize_mx(T.pairc[:], T.pairp[:], T.tpair[:]))
 
+    def send_f(k, at, codes, plane, a, sem):
+        send(k, u8(T.lc[:, at:at + CAPP]), u8(codes[:, a:a + CAPP]), sem)
+        send(k, T.lp[:, at:at + CAPP], plane[:, a:a + CAPP], sem)
+
     wait("g", v_qo)
-    c = a_col(opp, r)
-    send(opp, u8(T.lac[:, c:c + CAPP]), u8(T.oppc[:, 0:CAPP]), "f_opp")
-    send(opp, T.lap[:, c:c + CAPP], T.oppp[:, 0:CAPP], "f_opp")
+    send_f(opp, L_OPP, T.oppc, T.oppp, 0, "f_opp")
     wait("g", v_qp)
-    c = CAPP * (POS[r] % 2)
-    send_two([(nxt, u8(T.lbc[:, c:c + CAPP]), u8(T.pairc[:, 0:CAPP]), "f_prev"),
-              (prv, u8(T.lbc[:, c:c + CAPP]), u8(T.pairc[:, CAPP:H]), "f_next")])
-    send_two([(nxt, T.lbp[:, c:c + CAPP], T.pairp[:, 0:CAPP], "f_prev"),
-              (prv, T.lbp[:, c:c + CAPP], T.pairp[:, CAPP:H], "f_next")])
+    send_f(nxt, L_PREV, T.pairc, T.pairp, 0, "f_prev")
+    send_f(prv, L_NEXT, T.pairc, T.pairp, CAPP, "f_next")
 
     wait("A", v_w16)
     wait("V", v_w16)
-    ev = gather(T.tself, s0, CAPP, T.w16[:, 6 * r:6 * r + 6])
-    wait("V", v_p2, *ev)
-    c = a_col(r, r) - (PAD if s0 else 0)
-    v_qs = done(V.quantize_mx(T.lac[:, c:c + 128], T.lap[:, c:c + 128], T.tself[:]))
-    wait("V", *a_e)
-    v_qe = done(V.quantize_mx(T.ec[:], T.ep[:], T.et[:]))
+    ev = gather(T.tself, 4 * PAD, CAPP, T.w16[:, 6 * r:6 * r + 6])
+    wait("V", v_pad[1], v_pad[2], *ev)
+    v_qs = done(V.quantize_mx(T.lc[:, L_SELF - PAD:L_PREV], T.lp[:, L_SELF - PAD:L_PREV], T.tself[:]))
     wait("A", v_own)
     wait("V", v_own)
     ev_x = {}
-    for tile, h in ((T.xa, ha), (T.xb, hb)):
-        off = T.own16[:, 12 * h:12 * h + 12]
-        ev_x[h] = [done(V.tensor_scalar(tile[:, H * t:H * t + H], xwin(t).indirect(off), 0.5, None, mult)) if t < 2
+    for h in (ha, hb):
+        tile, off = T["xh%d" % h], T.own16[:, 12 * h:12 * h + 12]
+        ev_x[h] = [done(V.tensor_scalar(tile[:, H * t:H * t + H], xwin(t).indirect(off), 0.5, None, mult)) if t < 2 and h == ha
                    else done(A.activation(tile[:, H * t:H * t + H], xwin(t).indirect(off), COPY, scale=0.5))
                    for t in range(4)]
-    wait("V", e_w)
-    v_qw = done(V.quantize_mx(T.wc[:], T.wp[:], T.ws[:]))
 
-    v_m, v_qm = {}, {}
-    for h, lc, lp, base, arr, xh, mt, bank in (
-            (ha, T.lac, T.lap, a_base(r), [v_qs, ("f_opp", 2 * ne)], T.xa, T.ma, 0),
-            (hb, T.lbc, T.lbp, 0, [("f_next", ne), ("f_prev", ne)], T.xb, T.mb, 4)):
-        wait("PE", v_qe, *arr)
-        dec = [done(PE.matmul_mx(T["ps%d" % (bank + b)][:, 0:H], T.ec[:, 128 * b:128 * b + 128], T.ep[:, 128 * b:128 * b + 128],
-                                 lc[:, base:base + H], lp[:, base:base + H], True, True)) for b in range(4)]
-        v_m[h] = []
+    v_m, v_q = {}, {}
+    PAIR = ((nxt, T.prevc, T.prevp, "m_prev"), (prv, T.nextc, T.nextp, "m_next"))
+    for q, at, skip, arr, bank in ((r, L_SELF, 0, v_qs, 0), (opp, L_OPP, 0, ("f_opp", 2 * ne), 4),
+                                   (prv, L_PREV - PAD, PAD, ("f_prev", 2 * ne), 0),
+                                   (nxt, L_NEXT - PAD, PAD, ("f_next", 2 * ne), 4)):
+        h, c = POS[q] // 2, CAPP * (POS[q] % 2)
+        in_a = h == ha
+        mt, e0, xh = T.ma if in_a else T.mb, 4 * (c + (M_A if in_a else 0)), T["xh%d" % h]
+        wait("PE", v_qe, v_qs, arr)
+        v_m[q] = []
+        before = {prv: r, nxt: opp}.get(q)
+        dec = []
+        for b in range(4):
+            if before is not None:
+                wait("PE", v_m[before][b])
+            dec.append(done(PE.matmul_mx(T["ps%d" % (bank + b)][:, 0:128], T.ec[:, 128 * b:128 * b + 128], T.ep[:, 128 * b:128 * b + 128],
+                                         T.lc[:, at:at + 128], T.lp[:, at:at + 128], True, True)))
         for b in range(4):
             wait("V", dec[b], ev_x[h][b])
-            v_m[h].append(done(V.tensor_tensor(mt[:, b:4 * H:4], T["ps%d" % (bank + b)][:, 0:H], xh[:, H * b:H * b + H], add)))
-        wait("V", *v_m[h])
-        v_qm[h] = done(V.quantize_mx(T.mc[:, H * h:H * h + H], T.mp[:, H * h:H * h + H], mt[:]))
-        wait("g", v_qm[h])
-        m = slice(H * h, H * h + H)
-        k = 0 if h == ha else 1
-        for src, on, op in ((u8(T.mc[:, m]), u8(T.prevc[:, m]), u8(T.nextc[:, m])), (T.mp[:, m], T.prevp[:, m], T.nextp[:, m])):
-            send_two([(nxt, on, src, "m_prev%d" % k), (prv, op, src, "m_next%d" % k)])
+            v_m[q].append(done(V.tensor_tensor(mt[:, e0 + b:e0 + 4 * CAPP:4], T["ps%d" % (bank + b)][:, skip:skip + CAPP],
+                                               xh[:, H * b + c:H * b + c + CAPP], add)))
+        if in_a:
+            a = 128 if c else 0
+            wait("V", v_pad[3], v_pad[4], *v_m[q])
+            v_q[q] = done(V.quantize_mx(T.mc[:, a:a + 128], T.mp[:, a:a + 128], mt[:, 4 * a:4 * a + 512]))
+            wait("g", v_q[q])
+            a = M_A + c
+            send_two([(k, u8(lc[:, A_IN + c:A_IN + c + CAPP]), u8(T.mc[:, a:a + CAPP]), sem + "0") for k, lc, lp, sem in PAIR])
+        elif q == nxt:
+            wait("V", *v_m[prv], *v_m[nxt])
+            v_q[q] = done(V.quantize_mx(T.mc[:, M_B:M_ALL], T.mp[:, M_B:M_ALL], mt[:]))
+            wait("g", v_q[q])
+            for k, lc, lp, sem in PAIR:
+                send(k, lp[:], T.mp[:, M_A:M_ALL], sem + "p")
+                send(k, u8(lc[:, B_IN:IN_ALL]), u8(T.mc[:, M_B:M_ALL]), sem + "1")
 
     def product(bank, codes, plane, a, n):
         return done(PE.matmul_mx(T["ps%d" % bank][:, 0:n], T.wc[:], T.wp[:], codes[:, a:a + n], plane[:, a:a + n], True, True))
 
-    wait("PE", v_qw, v_m[ha][2], v_qm[ha], v_qm[hb])
-    p_own = product(2, T.mc, T.mp, 0, 2 * H)
-    wait("A", p_own)
-    a_own = done(A.activation(T.yw1[:], T.ps2[:, 0:2 * H], COPY))
-    wait("A", a_own, v_p16)
-    a_y1 = done(A.activation(T.ys1[:], T.yw1[:].indirect(T.pos16[:]), COPY))
+    def copy(q, out, src):
+        return done(V.tensor_copy(out, src) if q == "V" else A.activation(out, src, COPY))
+
+    wait("PE", v_qw, v_m[prv][2], v_m[nxt][2], v_q[r], v_q[opp], v_q[nxt])
+    p = [product(2, T.mc, T.mp, M_A, H), product(6, T.mc, T.mp, M_B, H)]
+    wait("A", *p)
+    a_own = [copy("A", T.yw1[:, H * ha:H * ha + H], T.ps2[:, 0:H]), copy("A", T.yw1[:, H * hb:H * hb + H], T.ps6[:, 0:H])]
+    wait("A", v_p16, *a_own)
+    a_y1 = copy("A", T.ys1[:], T.yw1[:].indirect(T.pos16[:]))
     wait("SY", a_y1)
     load(SY, T.y[:, S:2 * S], T.ys1[:], e_y)
-    cop = {"V": [], "A": []}
-    for k, h in ((0, hb), (1, ha)):
-        bank = 4 * k
-        for q, b, codes, plane, sem, win in (("V", bank, T.prevc, T.prevp, "m_prev%d" % k, T.yw0),
-                                             ("A", bank + 1, T.nextc, T.nextp, "m_next%d" % k, T.yw2)):
-            wait("PE", v_m[hb if k else ha][b % 4], (sem, ne))
-            p = product(b, codes, plane, H * h, H)
-            wait(q, p)
-            out, src = win[:, H * h:H * h + H], T["ps%d" % b][:, 0:H]
-            cop[q].append(done(V.tensor_copy(out, src) if q == "V" else A.activation(out, src, COPY)))
-    wait("V", ("p_prev", ne // 2), *cop["V"])
-    v_y0 = done(V.tensor_copy(T.ys0[:], T.yw0[:].indirect(T.pprev[:])))
-    wait("SY", v_y0)
-    load(SY, T.y[:, 0:S], T.ys0[:], e_y)
-    wait("A", ("p_next", ne // 2), *cop["A"])
-    a_y2 = done(A.activation(T.ys2[:], T.yw2[:].indirect(T.pnext[:]), COPY))
-    wait("A", a_y2)
-    load(A, T.y[:, 2 * S:3 * S], T.ys2[:], e_y)
+    o = H * hb
+    wait("PE", v_m[prv][0], ("m_prev0", ne), ("m_prevp", ne))
+    p = product(0, T.prevc, T.prevp, A_IN, H)
+    wait("V", p)
+    c_prev = [copy("V", T.yw0[:, o:o + H], T.ps0[:, 0:H])]
+
+    def finish(win, out, at, off, sem, copies, right):
+        for q, j, sq in (("V", 0, "SY"), ("A", 1, right)):
+            wait(q, (sem, nh), *copies)
+            e = copy(q, out[:, 128 * j:128 * j + 128], win[:].indirect(off[:, 8 * j:8 * j + 8]))
+            wait(sq, e)
+            load(queues[sq], T.y[:, at + 128 * j:at + 128 * j + 128], out[:, 128 * j:128 * j + 128], e_y)
+
+    o = H * ha
+    wait("PE", v_m[prv][3], ("m_prev1", ne))
+    p = product(3, T.prevc, T.prevp, B_IN, H)
+    wait("V", p)
+    c_prev.append(copy("V", T.yw0[:, o:o + H], T.ps3[:, 0:H]))
+    finish(T.yw0, T.ys0, 0, T.pprev, "p_prev", c_prev, "SY")
+    o = H * hb
+    wait("PE", v_m[prv][1], ("m_next0", ne), ("m_nextp", ne))
+    p = product(1, T.nextc, T.nextp, A_IN, H)
+    wait("A", p)
+    c_next = [copy("A", T.yw2[:, o:o + H], T.ps1[:, 0:H])]
+    o = H * ha
+    wait("PE", v_m[nxt][0], v_m[nxt][1], ("m_next1", ne))
+    p = [product(4, T.nextc, T.nextp, B_IN, 128), product(5, T.nextc, T.nextp, B_IN + H - 128, 128)]
+    wait("V", p[0])
+    c_next.append(copy("V", T.yw2[:, o:o + CAPP], T.ps4[:, 0:CAPP]))
+    wait("A", p[1])
+    c_next.append(copy("A", T.yw2[:, o + CAPP:o + H], T.ps5[:, PAD:128]))
+    finish(T.yw2, T.ys2, 2 * S, T.pnext, "p_next", c_next, "A")
 
     wait("g", e_y, ("sent", sent[0]))
     wait("g", *list(unwaited.items()))

@@ -2,48 +2,47 @@ from concourse.bass import DstId, RemoteDMATransfer
 from concourse.mybir import dt, AluOpType, ActivationFunctionType
 
 N, S, CAPP, R = 4, 256, 96, 1024
-POS = [0, 3, 1, 2]
-H = 2 * CAPP
+SLOTS = N * CAPP
 PAD = 128 - CAPP
 F8 = "float8_e4m3fn_x4"
-L_OPP, L_SELF, L_PREV, L_NEXT, L_ALL = 0, 128, 256, 352, 448
-M_A, M_B, M_ALL = PAD, H + 2 * PAD, 2 * H + 2 * PAD
-A_IN, B_IN, IN_ALL = 0, M_B - PAD, M_ALL - PAD
+L_OPP, L_PREV, L_SELF, L_NEXT, L_ALL = 0, CAPP, 2 * CAPP, 3 * CAPP + PAD, 4 * CAPP + PAD
+M_ALL = SLOTS + PAD
 
 SCRATCH = {
     "xs": ("sbuf", [128, 4 * R], "bfloat16"),
     "ws": ("sbuf", [128, 512], "bfloat16"),
     "wl": ("sbuf", [128, 24], "int32"), "sl": ("sbuf", [128, 16], "int32"), "ol": ("sbuf", [128, 256], "int32"),
     "w16": ("sbuf", [128, 24], "uint16"),
-    "lopp": ("sbuf", [128, 6], "uint16"), "lpair": ("sbuf", [128, 12], "uint16"),
+    "lopp": ("sbuf", [128, 6], "uint16"), "lnext": ("sbuf", [128, 6], "uint16"), "lprev": ("sbuf", [128, 6], "uint16"),
     "u1": ("sbuf", [128, 16], "int32"), "u2": ("sbuf", [128, 16], "int32"), "u3": ("sbuf", [128, 16], "int32"),
-    "pos": ("sbuf", [128, 16], "int32"),
     "pos16": ("sbuf", [128, 16], "uint16"), "pprev": ("sbuf", [128, 16], "uint16"), "pnext": ("sbuf", [128, 16], "uint16"),
     "so": ("sbuf", [128, 32], "float32"), "sot": ("sbuf", [128, 32], "float32"), "so16": ("sbuf", [128, 16], "uint16"),
-    "flat": ("sbuf", [128, 416], "float32"), "flatt": ("sbuf", [128, 416], "float32"),
-    "sel": ("sbuf", [128, 48], "float32"), "ownf": ("sbuf", [128, 24], "float32"), "own16": ("sbuf", [128, 24], "uint16"),
-    "pidx": ("sbuf", [128, 1], "int32"), "podd": ("sbuf", [128, 1], "int32"),
-    "odd16": ("sbuf", [128, 1], "float32"), "modd": ("sbuf", [128, 1], "float32"), "meven": ("sbuf", [128, 1], "float32"),
+    "flat": ("sbuf", [128, SLOTS], "float32"), "ownf": ("sbuf", [128, 24], "float32"), "own16": ("sbuf", [128, 24], "uint16"),
     "half": ("sbuf", [128, 512], "bfloat16"), "ident": ("sbuf", [128, 128], "bfloat16"),
     "et": ("sbuf", [128, 2048], "bfloat16"), "ec": ("sbuf", [128, 512], F8), "ep": ("sbuf", [128, 512], "uint8"),
     "wc": ("sbuf", [128, 128], F8), "wp": ("sbuf", [128, 128], "uint8"),
-    "topp": ("sbuf", [128, 512], "bfloat16"), "tself": ("sbuf", [128, 640], "bfloat16"), "tpair": ("sbuf", [128, 4 * H], "bfloat16"),
-    "oppc": ("sbuf", [128, 128], F8), "oppp": ("sbuf", [128, 128], "uint8"),
-    "pairc": ("sbuf", [128, H], F8), "pairp": ("sbuf", [128, H], "uint8"),
+    "tself": ("sbuf", [128, 512], "bfloat16"),
     "lc": ("sbuf", [128, L_ALL], F8), "lp": ("sbuf", [128, L_ALL], "uint8"),
-    "xh0": ("sbuf", [128, 4 * H], "bfloat16"), "xh1": ("sbuf", [128, 4 * H], "bfloat16"),
-    "ma": ("sbuf", [128, 4 * M_B], "bfloat16"), "mb": ("sbuf", [128, 4 * H], "bfloat16"),
     "mc": ("sbuf", [128, M_ALL], F8), "mp": ("sbuf", [128, M_ALL], "uint8"),
-    "prevc": ("sbuf", [128, IN_ALL], F8), "prevp": ("sbuf", [128, IN_ALL], "uint8"),
-    "nextc": ("sbuf", [128, IN_ALL], F8), "nextp": ("sbuf", [128, IN_ALL], "uint8"),
-    "yw0": ("sbuf", [128, 2 * H], "float32"), "yw1": ("sbuf", [128, 2 * H], "float32"), "yw2": ("sbuf", [128, 2 * H], "float32"),
-    "ys0": ("sbuf", [128, S], "float32"), "ys1": ("sbuf", [128, S], "float32"), "ys2": ("sbuf", [128, S], "float32"),
+    "prevc": ("sbuf", [128, SLOTS], F8), "prevp": ("sbuf", [128, SLOTS], "uint8"),
+    "nextc": ("sbuf", [128, SLOTS], F8), "nextp": ("sbuf", [128, SLOTS], "uint8"),
 }
+for _k in ("next", "prev", "opp"):
+    SCRATCH["t" + _k] = ("sbuf", [128, 512], "bfloat16")
+    SCRATCH["c" + _k] = ("sbuf", [128, 128], F8)
+    SCRATCH["s" + _k] = ("sbuf", [128, 128], "uint8")
+for _k in range(2):
+    SCRATCH["xh%d" % _k] = ("sbuf", [128, 8 * CAPP], "bfloat16")
+for _k in range(4):
+    SCRATCH["mt%d" % _k] = ("sbuf", [128, 512], "bfloat16")
+for _k in range(3):
+    SCRATCH["yw%d" % _k] = ("sbuf", [128, SLOTS], "float32")
+    SCRATCH["ys%d" % _k] = ("sbuf", [128, S], "float32")
 for _k in range(8):
     SCRATCH["ps%d" % _k] = ("psum", [128, 512], "float32")
 ARR = ["sent", "l_opp", "l_next", "l_prev", "p_next", "p_prev", "f_opp", "f_next", "f_prev",
-       "m_next0", "m_next1", "m_prev0", "m_prev1", "m_nextp", "m_prevp"]
-SEMAPHORES = ARR + ["e%d" % _k for _k in range(132)]
+       "m_next0", "m_next1", "m_next2", "m_next3", "m_nextp", "m_prev0", "m_prev1", "m_prev2", "m_prev3", "m_prevp"]
+SEMAPHORES = ARR + ["e%d" % _k for _k in range(130)]
 
 
 def rank_program(g, core, T, topo):
@@ -77,9 +76,6 @@ def rank_program(g, core, T, topo):
         ins.then_inc(T.sem[e[0]], n)
         return e
 
-    ha = POS[r] // 2
-    hb = 1 - ha
-
     sent = [0]
 
     def engs(k):
@@ -108,7 +104,7 @@ def rank_program(g, core, T, topo):
     def u8(v):
         return v.bitcast(dt.uint8)
 
-    e_want, e_slot, e_own, e_x, e_w, e_y = event(128), event(128), event(128), event(16), event(16), event(80)
+    e_want, e_slot, e_own, e_x, e_w, e_of, e_y = (event(128), event(128), event(16), event(16), event(16), event(128), event(80))
 
     def load(q, out, src, e):
         q.dma_start(out, src).then_inc(T.sem[e[0]], 16)
@@ -116,33 +112,28 @@ def rank_program(g, core, T, topo):
     for k in range(4):
         load(SY, T.wl[16 * k:16 * k + 16, :], T.want[:], e_want)
         load(A, T.wl[16 * k + 64:16 * k + 80, :], T.want[:], e_want)
+    for k in range(4):
+        load(SY, T.sl[16 * k:16 * k + 16, :], T.slot[:], e_slot)
+        load(A, T.sl[16 * k + 64:16 * k + 80, :], T.slot[:], e_slot)
     load(SY, T.xs[:], T.x[:], e_x)
-    for k in range(8):
-        load(A, T.sl[16 * k:16 * k + 16, :], T.slot[:], e_slot)
 
-    g_p = done(g.iota(T.pidx[:], [[1, 1]], 0, 1))
     v_ol = done(V.memset(T.ol[:], 0))
     v_half = done(V.memset(T.half[:], 0.5))
-    v_pad = [done(V.memset(T.topp[:, 4 * CAPP:512], 0.0)), done(V.memset(T.tself[:, 0:4 * PAD], 0.0)),
-             done(V.memset(T.tself[:, 512:640], 0.0)), done(V.memset(T.ma[:, 0:4 * M_A], 0.0)),
-             done(V.memset(T.ma[:, 4 * (M_B - PAD):4 * M_B], 0.0))]
-    wait("V", g_p)
-    v_odd = done(V.tensor_scalar(T.podd[:], T.pidx[:], 16, None, AluOpType.bitwise_and))
-    wait("V", v_odd)
-    v_o16 = done(V.tensor_copy(T.odd16[:], T.podd[:]))
+    v_pad = {k: done(V.memset(T["t" + k][:, 4 * CAPP:512], 0.0)) for k in ("next", "prev", "opp", "self")}
+    v_mpad = [done(V.memset(T["mt%d" % i][:, 4 * CAPP:512], 0.0)) for i in range(4)]
+    z = [done(V.memset(T.et[:, 512 * b:512 * b + 512], 0.0)) for b in (0, 1)]
     wait("A", v_ol)
-    for k in range(8):
-        load(A, T.ol[16 * k:16 * k + 1, :], T.own[:], e_own)
+    load(A, T.ol[0:1, :], T.own[:], e_own)
     load(A, T.ws[:], T.w[:], e_w)
     wait("g", v_half)
     g_id = done(g.affine_select(T.ident[:], T.half[:, 0:128], [[-1, 128]], AluOpType.is_equal, 0.0, 0, 1))
     wait("A", v_half)
-    a_flat = done(A.activation(T.flat[:], T.half[:, 0:416], COPY, scale=0.0))
-    a_z = [done(A.activation(T.et[:, 512 * b:512 * b + 512], T.half[:], COPY, scale=0.0)) for b in range(4)]
+    a_flat = done(A.activation(T.flat[:], T.half[:, 0:SLOTS], COPY, scale=0.0))
+    z += [done(A.activation(T.et[:, 512 * b:512 * b + 512], T.half[:], COPY, scale=0.0)) for b in (2, 3)]
     wait("A", g_id)
     a_e = []
     for b in range(4):
-        wait("A", a_z[b])
+        wait("A", z[b])
         a_e.append(done(A.activation(T.et[:, 512 * b + b:512 * b + 512:4], T.ident[:], COPY)))
 
     wait("V", e_want)
@@ -152,123 +143,103 @@ def rank_program(g, core, T, topo):
     def wcols(k):
         return T.w16[:, 6 * k:6 * k + 6]
 
+    send_two([(nxt, T.lprev[:], wcols(nxt), "l_prev"), (prv, T.lnext[:], wcols(prv), "l_next")])
     send(opp, T.lopp[:], wcols(opp), "l_opp")
-    send_two([(nxt, T.lpair[:, 6:12], wcols(nxt), "l_prev"), (prv, T.lpair[:, 0:6], wcols(prv), "l_next")])
 
     wait("V", e_slot)
-    v1 = done(V.tensor_scalar(T.u1[:], T.sl[:], CAPP, 2 * CAPP, AluOpType.is_ge, mult))
-    v2 = done(V.tensor_scalar(T.u2[:], T.sl[:], 2 * CAPP, -3 * CAPP, AluOpType.is_ge, mult))
-    wait("V", v1, v2)
-    v3 = done(V.tensor_tensor(T.u3[:], T.u1[:], T.u2[:], add))
-    wait("V", v3)
-    v_s = [done(V.tensor_tensor(T.so[:, 16 * j:16 * j + 16], T.sl[:], T.u3[:], add)) for j in range(2)]
-    v_pos = done(V.tensor_tensor(T.pos[:], T.sl[:], T.u3[:], add))
-    wait("V", *v_s)
-    v_t = done(V.transpose(T.sot[:], T.so[:]))
-    wait("V", v_pos)
-    v_p16 = done(V.tensor_copy(T.pos16[:], T.pos[:]))
+    v1 = done(V.tensor_scalar(T.u1[:], T.sl[:], 4, None, AluOpType.arith_shift_right))
+    v2 = done(V.tensor_scalar(T.u2[:], T.sl[:], 24, None, mult))
+    v_p16 = done(V.tensor_copy(T.pos16[:], T.sl[:]))
+    wait("V", v1)
+    v3 = done(V.tensor_scalar(T.u3[:], T.u1[:], 1 - SLOTS, None, mult))
     wait("g", v_p16)
     send_two([(nxt, T.pprev[:], T.pos16[:], "p_prev"), (prv, T.pnext[:], T.pos16[:], "p_next")])
-    wait("V", v_t, v_o16)
-    v_o = done(V.tensor_scalar(T.so16[:], T.sot[:, 0:16], T.odd16[:], None, add))
-    v_mask = [done(V.tensor_scalar(T.modd[:], T.odd16[:], 0.25, None, mult)),
-              done(V.tensor_scalar(T.meven[:], T.odd16[:], -0.25, 4.0, mult, add))]
+    wait("V", v2, v3)
+    v_s = [done(V.tensor_tensor(T.so[:, 16 * j:16 * j + 16], T.u2[:], T.u3[:], add)) for j in range(2)]
+    wait("V", *v_s)
+    v_t = done(V.transpose(T.sot[:], T.so[:]))
+    wait("V", v_t)
+    v_o = done(V.tensor_copy(T.so16[:], T.sot[:, 0:16]))
     wait("V", e_own, a_flat, v_o)
     v_sc = done(V.tensor_copy(T.flat[:].indirect(T.so16[:]), T.ol[:]))
-    wait("V", v_sc, *v_mask)
-    v_ft = done(V.transpose(T.flatt[:], T.flat[:]))
-    wait("V", v_ft)
-    v_sel = [done(V.tensor_scalar(T.sel[:, 12 * j:12 * j + 12], T.flatt[:, a:e:32], m[:], None, mult))
-             for j, (a, e, m) in enumerate(((0, 384, T.meven), (16, 384, T.modd), (48, 416, T.meven), (0, 384, T.modd)))]
-    wait("V", *v_sel)
-    v_of = [done(V.tensor_tensor(T.ownf[:, j:24:2], T.sel[:, 24 * j:24 * j + 12], T.sel[:, 24 * j + 12:24 * j + 24], add)) for j in range(2)]
-    wait("V", *v_of)
-    v_own = done(V.tensor_copy(T.own16[:], T.ownf[:]))
-    wait("V", *a_e)
-    v_qe = done(V.quantize_mx(T.ec[:], T.ep[:], T.et[:]))
-    wait("V", e_w)
-    v_qw = done(V.quantize_mx(T.wc[:], T.wp[:], T.ws[:]))
+    wait("SY", v_sc)
+    for k in range(8):
+        load(SY, T.ownf[16 * k:16 * k + 16, :], T.flat[0:1, :], e_of)
 
     def xwin(t):
         return T.xs[:, t:4 * R]
 
-    def gather(tile, a, n, off):
+    def gather(tile, off):
         ev = []
         for t in range(4):
-            out, src = tile[:, a + t:a + 4 * n:4], xwin(t).indirect(off)
+            out, src = tile[:, t:4 * CAPP:4], xwin(t).indirect(off)
             ev.append(done(V.tensor_copy(out, src)) if t < 2 else done(A.activation(out, src, COPY)))
         return ev
 
+    wait("V", *a_e)
+    v_qe = done(V.quantize_mx(T.ec[:], T.ep[:], T.et[:]))
     for q in ("V", "A"):
-        wait(q, e_x, ("l_opp", ne))
-    ev = gather(T.topp, 0, CAPP, T.lopp[:])
-    wait("V", v_pad[0], *ev)
-    v_qo = done(V.quantize_mx(T.oppc[:], T.oppp[:], T.topp[:]))
+        wait(q, e_x, v_w16)
+    ev = gather(T.tself, wcols(r))
+    wait("V", v_pad["self"], *ev)
+    v_qs = done(V.quantize_mx(T.lc[:, L_SELF:L_SELF + 128], T.lp[:, L_SELF:L_SELF + 128], T.tself[:]))
+    for k, name, back, at, n in ((nxt, "next", "f_prev", L_PREV, nh), (prv, "prev", "f_next", L_NEXT, nh),
+                                 (opp, "opp", "f_opp", L_OPP, ne)):
+        for q in ("V", "A"):
+            wait(q, ("l_" + name, n))
+        ev = gather(T["t" + name], T["l" + name][:])
+        wait("V", v_pad[name], *ev)
+        e = done(V.quantize_mx(T["c" + name][:], T["s" + name][:], T["t" + name][:]))
+        wait("g", e)
+        send(k, u8(T.lc[:, at:at + CAPP]), u8(T["c" + name][:, 0:CAPP]), back)
+        send(k, T.lp[:, at:at + CAPP], T["s" + name][:, 0:CAPP], back)
+
+    wait("V", e_of)
+    v_own = done(V.tensor_scalar(T.own16[:], T.ownf[:], 4, None, mult))
     for q in ("V", "A"):
-        wait(q, ("l_next", nh), ("l_prev", nh))
-    ev = gather(T.tpair, 0, H, T.lpair[:])
-    wait("V", *ev)
-    v_qp = done(V.quantize_mx(T.pairc[:], T.pairp[:], T.tpair[:]))
+        wait(q, v_own)
 
-    def send_f(k, at, codes, plane, a, sem):
-        send(k, u8(T.lc[:, at:at + CAPP]), u8(codes[:, a:a + CAPP]), sem)
-        send(k, T.lp[:, at:at + CAPP], plane[:, a:a + CAPP], sem)
+    def own_columns(h, t, q):
+        out, src = T["xh%d" % h][:, 2 * CAPP * t:2 * CAPP * t + 2 * CAPP], xwin(t).indirect(T.own16[:, 12 * h:12 * h + 12])
+        return done(V.tensor_scalar(out, src, 0.5, None, mult) if q == "V" else A.activation(out, src, COPY, scale=0.5))
 
-    wait("g", v_qo)
-    send_f(opp, L_OPP, T.oppc, T.oppp, 0, "f_opp")
-    wait("g", v_qp)
-    send_f(nxt, L_PREV, T.pairc, T.pairp, 0, "f_prev")
-    send_f(prv, L_NEXT, T.pairc, T.pairp, CAPP, "f_next")
-
-    wait("A", v_w16)
-    wait("V", v_w16)
-    ev = gather(T.tself, 4 * PAD, CAPP, T.w16[:, 6 * r:6 * r + 6])
-    wait("V", v_pad[1], v_pad[2], *ev)
-    v_qs = done(V.quantize_mx(T.lc[:, L_SELF - PAD:L_PREV], T.lp[:, L_SELF - PAD:L_PREV], T.tself[:]))
-    wait("A", v_own)
-    wait("V", v_own)
-    ev_x = {}
-    for h in (ha, hb):
-        tile, off = T["xh%d" % h], T.own16[:, 12 * h:12 * h + 12]
-        ev_x[h] = [done(V.tensor_scalar(tile[:, H * t:H * t + H], xwin(t).indirect(off), 0.5, None, mult)) if t < 2 and h == ha
-                   else done(A.activation(tile[:, H * t:H * t + H], xwin(t).indirect(off), COPY, scale=0.5))
-                   for t in range(4)]
+    ev_x = {r // 2: [own_columns(r // 2, t, "VVAA"[t]) for t in range(4)],
+            1 - r // 2: [own_columns(1 - r // 2, t, "A") for t in range(3)]}
 
     v_m, v_q = {}, {}
-    PAIR = ((nxt, T.prevc, T.prevp, "m_prev"), (prv, T.nextc, T.nextp, "m_next"))
-    for q, at, skip, arr, bank in ((r, L_SELF, 0, v_qs, 0), (opp, L_OPP, 0, ("f_opp", 2 * ne), 4),
-                                   (prv, L_PREV - PAD, PAD, ("f_prev", 2 * ne), 0),
-                                   (nxt, L_NEXT - PAD, PAD, ("f_next", 2 * ne), 4)):
-        h, c = POS[q] // 2, CAPP * (POS[q] % 2)
-        in_a = h == ha
-        mt, e0, xh = T.ma if in_a else T.mb, 4 * (c + (M_A if in_a else 0)), T["xh%d" % h]
-        wait("PE", v_qe, v_qs, arr)
-        v_m[q] = []
-        before = {prv: r, nxt: opp}.get(q)
-        dec = []
+    for i, (q, at, skip, arr) in enumerate(((r, L_SELF, 0, v_qs), (prv, L_PREV, 0, ("f_prev", 2 * ne)),
+                                            (nxt, L_NEXT - PAD, PAD, ("f_next", 2 * ne)),
+                                            (opp, L_OPP, 0, ("f_opp", 2 * ne)))):
+        bank, h, c = 4 * (i % 2), q // 2, CAPP * (q % 2)
+        m0 = CAPP * i
+        wait("PE", v_qe, arr)
+        dec, v_m[i] = [], []
         for b in range(4):
-            if before is not None:
-                wait("PE", v_m[before][b])
+            if i > 1:
+                wait("PE", v_m[i - 2][b])
             dec.append(done(PE.matmul_mx(T["ps%d" % (bank + b)][:, 0:128], T.ec[:, 128 * b:128 * b + 128], T.ep[:, 128 * b:128 * b + 128],
                                          T.lc[:, at:at + 128], T.lp[:, at:at + 128], True, True)))
         for b in range(4):
             wait("V", dec[b], ev_x[h][b])
-            v_m[q].append(done(V.tensor_tensor(mt[:, e0 + b:e0 + 4 * CAPP:4], T["ps%d" % (bank + b)][:, skip:skip + CAPP],
-                                               xh[:, H * b + c:H * b + c + CAPP], add)))
-        if in_a:
-            a = 128 if c else 0
-            wait("V", v_pad[3], v_pad[4], *v_m[q])
-            v_q[q] = done(V.quantize_mx(T.mc[:, a:a + 128], T.mp[:, a:a + 128], mt[:, 4 * a:4 * a + 512]))
-            wait("g", v_q[q])
-            a = M_A + c
-            send_two([(k, u8(lc[:, A_IN + c:A_IN + c + CAPP]), u8(T.mc[:, a:a + CAPP]), sem + "0") for k, lc, lp, sem in PAIR])
-        elif q == nxt:
-            wait("V", *v_m[prv], *v_m[nxt])
-            v_q[q] = done(V.quantize_mx(T.mc[:, M_B:M_ALL], T.mp[:, M_B:M_ALL], mt[:]))
-            wait("g", v_q[q])
-            for k, lc, lp, sem in PAIR:
-                send(k, lp[:], T.mp[:, M_A:M_ALL], sem + "p")
-                send(k, u8(lc[:, B_IN:IN_ALL]), u8(T.mc[:, M_B:M_ALL]), sem + "1")
+            v_m[i].append(done(V.tensor_tensor(T["mt%d" % i][:, b:4 * CAPP:4], T["ps%d" % (bank + b)][:, skip:skip + CAPP],
+                                               T["xh%d" % h][:, 2 * CAPP * b + c:2 * CAPP * b + c + CAPP], add)))
+        wait("V", v_mpad[i], *v_m[i])
+        if i:
+            wait("V", v_q[i - 1])
+        v_q[i] = done(V.quantize_mx(T.mc[:, m0:m0 + 128], T.mp[:, m0:m0 + 128], T["mt%d" % i][:]))
+        wait("g", v_q[i])
+        two = [(k, u8(land[:, m0:m0 + CAPP]), u8(T.mc[:, m0:m0 + CAPP]), "m_%s%d" % (name, i))
+               for k, land, name in ((nxt, T.prevc, "prev"), (prv, T.nextc, "next"))]
+        if i < 3:
+            send_two(two)
+        else:
+            send_two([(nxt, T.prevp[:], T.mp[:, 0:SLOTS], "m_prevp"), (prv, T.nextp[:], T.mp[:, 0:SLOTS], "m_nextp")])
+            for w in two:
+                send(*w)
+        if i == 0:
+            ev_x[1 - r // 2].append(own_columns(1 - r // 2, 3, "V"))
+    wait("V", e_w)
+    v_qw = done(V.quantize_mx(T.wc[:], T.wp[:], T.ws[:]))
 
     def product(bank, codes, plane, a, n):
         return done(PE.matmul_mx(T["ps%d" % bank][:, 0:n], T.wc[:], T.wp[:], codes[:, a:a + n], plane[:, a:a + n], True, True))
@@ -276,46 +247,40 @@ def rank_program(g, core, T, topo):
     def copy(q, out, src):
         return done(V.tensor_copy(out, src) if q == "V" else A.activation(out, src, COPY))
 
-    wait("PE", v_qw, v_m[prv][2], v_m[nxt][2], v_q[r], v_q[opp], v_q[nxt])
-    p = [product(2, T.mc, T.mp, M_A, H), product(6, T.mc, T.mp, M_B, H)]
-    wait("A", *p)
-    a_own = [copy("A", T.yw1[:, H * ha:H * ha + H], T.ps2[:, 0:H]), copy("A", T.yw1[:, H * hb:H * hb + H], T.ps6[:, 0:H])]
+    def unload(q, win, s, bank, first, blocks):
+        order = (s, (s - 1) % N, (s + 1) % N, (s + 2) % N)
+        return [copy(q, win[:, CAPP * order[j]:CAPP * order[j] + CAPP], T["ps%d" % bank][:, CAPP * j - first:CAPP * j - first + CAPP])
+                for j in blocks]
+
+    def gather_out(q, out, win, off, j, n):
+        return copy(q, out[:, j:j + n], win[:].indirect(off[:, j // 16:(j + n) // 16]))
+
+    wait("PE", v_qw, *[e for i in v_m for e in v_m[i]], *[v_q[i] for i in v_q])
+    p = product(0, T.mc, T.mp, 0, SLOTS)
+    wait("A", p)
+    a_own = unload("A", T.yw1, r, 0, 0, range(4))
     wait("A", v_p16, *a_own)
-    a_y1 = copy("A", T.ys1[:], T.yw1[:].indirect(T.pos16[:]))
+    a_y1 = gather_out("A", T.ys1, T.yw1, T.pos16, 0, S)
     wait("SY", a_y1)
     load(SY, T.y[:, S:2 * S], T.ys1[:], e_y)
-    o = H * hb
-    wait("PE", v_m[prv][0], ("m_prev0", ne), ("m_prevp", ne))
-    p = product(0, T.prevc, T.prevp, A_IN, H)
-    wait("V", p)
-    c_prev = [copy("V", T.yw0[:, o:o + H], T.ps0[:, 0:H])]
-
-    def finish(win, out, at, off, sem, copies, right):
-        for q, j, sq in (("V", 0, "SY"), ("A", 1, right)):
-            wait(q, (sem, nh), *copies)
-            e = copy(q, out[:, 128 * j:128 * j + 128], win[:].indirect(off[:, 8 * j:8 * j + 8]))
+    sides = (("prev", prv, T.prevc, T.prevp, T.yw0), ("next", nxt, T.nextc, T.nextp, T.yw2))
+    copies = {}
+    for j, (name, s, c, pl, win) in enumerate(sides):
+        wait("PE", *[("m_%s%s" % (name, e), nh) for e in "012p"])
+        p = product(1 + j, c, pl, 0, 3 * CAPP)
+        wait("VA"[j], p)
+        copies[name] = unload("VA"[j], win, s, 1 + j, 0, range(3))
+    for j, (name, s, c, pl, win) in enumerate(sides):
+        wait("PE", ("m_%s3" % name, ne))
+        p = product(3 + j, c, pl, SLOTS - 128, 128)
+        wait("V", p)
+        copies[name] += unload("V", win, s, 3 + j, SLOTS - 128, (3,))
+        out, off, at = (T.ys0, T.pprev, 0) if j == 0 else (T.ys2, T.pnext, 2 * S)
+        for q, a, sq in (("V", 0, "SY"), ("A", 128, "A" if j else "SY")):
+            wait(q, ("p_" + name, nh), *copies[name])
+            e = gather_out(q, out, win, off, a, 128)
             wait(sq, e)
-            load(queues[sq], T.y[:, at + 128 * j:at + 128 * j + 128], out[:, 128 * j:128 * j + 128], e_y)
-
-    o = H * ha
-    wait("PE", v_m[prv][3], ("m_prev1", ne))
-    p = product(3, T.prevc, T.prevp, B_IN, H)
-    wait("V", p)
-    c_prev.append(copy("V", T.yw0[:, o:o + H], T.ps3[:, 0:H]))
-    finish(T.yw0, T.ys0, 0, T.pprev, "p_prev", c_prev, "SY")
-    o = H * hb
-    wait("PE", v_m[prv][1], ("m_next0", ne), ("m_nextp", ne))
-    p = product(1, T.nextc, T.nextp, A_IN, H)
-    wait("A", p)
-    c_next = [copy("A", T.yw2[:, o:o + H], T.ps1[:, 0:H])]
-    o = H * ha
-    wait("PE", v_m[nxt][0], v_m[nxt][1], ("m_next1", ne))
-    p = [product(4, T.nextc, T.nextp, B_IN, 128), product(5, T.nextc, T.nextp, B_IN + H - 128, 128)]
-    wait("V", p[0])
-    c_next.append(copy("V", T.yw2[:, o:o + CAPP], T.ps4[:, 0:CAPP]))
-    wait("A", p[1])
-    c_next.append(copy("A", T.yw2[:, o + CAPP:o + H], T.ps5[:, PAD:128]))
-    finish(T.yw2, T.ys2, 2 * S, T.pnext, "p_next", c_next, "A")
+            load(queues[sq], T.y[:, at + a:at + a + 128], out[:, a:a + 128], e_y)
 
     wait("g", e_y, ("sent", sent[0]))
     wait("g", *list(unwaited.items()))

from concourse.bass import DstId, RemoteDMATransfer
from concourse.mybir import dt, AluOpType, ActivationFunctionType

N, S, CAPP, R = 4, 256, 96, 1024
SLOTS = N * CAPP
PAD = 128 - CAPP
F8 = "float8_e4m3fn_x4"
L_OPP, L_PREV, L_SELF, L_NEXT, L_ALL = 0, CAPP, 2 * CAPP, 3 * CAPP + PAD, 4 * CAPP + PAD
M_ALL = SLOTS + PAD

SCRATCH = {
    "xs": ("sbuf", [128, 4 * R], "bfloat16"),
    "ws": ("sbuf", [128, 512], "bfloat16"),
    "wl": ("sbuf", [128, 24], "int32"), "sl": ("sbuf", [128, 16], "int32"), "ol": ("sbuf", [128, 256], "int32"),
    "w16": ("sbuf", [128, 24], "uint16"),
    "lopp": ("sbuf", [128, 6], "uint16"), "lnext": ("sbuf", [128, 6], "uint16"), "lprev": ("sbuf", [128, 6], "uint16"),
    "u1": ("sbuf", [128, 16], "int32"), "u2": ("sbuf", [128, 16], "int32"), "u3": ("sbuf", [128, 16], "int32"),
    "pos16": ("sbuf", [128, 16], "uint16"), "pprev": ("sbuf", [128, 16], "uint16"), "pnext": ("sbuf", [128, 16], "uint16"),
    "so": ("sbuf", [128, 32], "float32"), "sot": ("sbuf", [128, 32], "float32"), "so16": ("sbuf", [128, 16], "uint16"),
    "flat": ("sbuf", [128, SLOTS], "float32"), "ownf": ("sbuf", [128, 24], "float32"), "own16": ("sbuf", [128, 24], "uint16"),
    "half": ("sbuf", [128, 512], "bfloat16"), "ident": ("sbuf", [128, 128], "bfloat16"),
    "et": ("sbuf", [128, 2048], "bfloat16"), "ec": ("sbuf", [128, 512], F8), "ep": ("sbuf", [128, 512], "uint8"),
    "wc": ("sbuf", [128, 128], F8), "wp": ("sbuf", [128, 128], "uint8"),
    "tself": ("sbuf", [128, 512], "bfloat16"),
    "lc": ("sbuf", [128, L_ALL], F8), "lp": ("sbuf", [128, L_ALL], "uint8"),
    "mc": ("sbuf", [128, M_ALL], F8), "mp": ("sbuf", [128, M_ALL], "uint8"),
    "prevc": ("sbuf", [128, SLOTS], F8), "prevp": ("sbuf", [128, SLOTS], "uint8"),
    "nextc": ("sbuf", [128, SLOTS], F8), "nextp": ("sbuf", [128, SLOTS], "uint8"),
}
for _k in ("next", "prev", "opp"):
    SCRATCH["t" + _k] = ("sbuf", [128, 512], "bfloat16")
    SCRATCH["c" + _k] = ("sbuf", [128, 128], F8)
    SCRATCH["s" + _k] = ("sbuf", [128, 128], "uint8")
for _k in range(2):
    SCRATCH["xh%d" % _k] = ("sbuf", [128, 8 * CAPP], "bfloat16")
for _k in range(4):
    SCRATCH["mt%d" % _k] = ("sbuf", [128, 512], "bfloat16")
for _k in range(3):
    SCRATCH["yw%d" % _k] = ("sbuf", [128, SLOTS], "float32")
    SCRATCH["ys%d" % _k] = ("sbuf", [128, S], "float32")
for _k in range(8):
    SCRATCH["ps%d" % _k] = ("psum", [128, 512], "float32")
ARR = ["sent", "l_opp", "l_next", "l_prev", "p_next", "p_prev", "f_opp", "f_next", "f_prev",
       "m_next0", "m_next1", "m_next2", "m_next3", "m_nextp", "m_prev0", "m_prev1", "m_prev2", "m_prev3", "m_prevp"]
SEMAPHORES = ARR + ["e%d" % _k for _k in range(130)]


def rank_program(g, core, T, topo):
    r = T.rank_of(core)
    if r is None:
        return
    V, A, PE, SY = g.vector, g.scalar, g.tensor, g.sync
    queues = {"g": g, "V": V, "A": A, "PE": PE, "SY": SY}
    add, mult = AluOpType.add, AluOpType.mult
    COPY = ActivationFunctionType.Copy
    nxt, prv, opp = (r + 1) % N, (r - 1) % N, (r + 2) % N
    nevents = [0]
    seen = set()
    unwaited = {}

    def event(n=1):
        name = "e%d" % nevents[0]
        nevents[0] += 1
        unwaited[name] = n
        return (name, n)

    def wait(q, *evs):
        for name, n in evs:
            if (q, name) not in seen:
                seen.add((q, name))
                unwaited.pop(name, None)
                queues[q].wait_ge(T.sem[name], n)

    def done(ins, n=1):
        e = event(n)
        ins.then_inc(T.sem[e[0]], n)
        return e

    sent = [0]

    def engs(k):
        return topo.engines(core, T.cores[k])

    def send(k, out, src, sem):
        rid, pid, _ = topo.addr(T.cores[k])
        g.remote_dma(out_ap=out, in_ap=src, remote_sem=T.sem[sem], local_sem=T.sem.sent, pid=pid, routing_id=rid,
                     dma_engine_mask=topo.mask(core, T.cores[k]))
        sent[0] += len(engs(k))

    def send_two(items):
        tr = []
        for i, (k, out, src, sem) in enumerate(items):
            es = engs(k)
            es = es[i * len(es) // 2:(i + 1) * len(es) // 2]
            sent[0] += len(es)
            rid, pid, _ = topo.addr(T.cores[k])
            tr.append(RemoteDMATransfer(dst_ids=[DstId(rid=rid, pnc=pid)], dma_engine_mask=sum(1 << e for e in es),
                                        remote_sem=T.sem[sem], srcs=[src], dsts=[out]))
        g.remote_dma_fused(tr, local_sem=T.sem.sent)

    ne = len(engs(opp))
    nh = ne // 2

    def u8(v):
        return v.bitcast(dt.uint8)

    e_want, e_slot, e_own, e_x, e_w, e_of, e_y = (event(128), event(128), event(16), event(16), event(16), event(128), event(80))

    def load(q, out, src, e):
        q.dma_start(out, src).then_inc(T.sem[e[0]], 16)

    for k in range(4):
        load(SY, T.wl[16 * k:16 * k + 16, :], T.want[:], e_want)
        load(A, T.wl[16 * k + 64:16 * k + 80, :], T.want[:], e_want)
    for k in range(4):
        load(SY, T.sl[16 * k:16 * k + 16, :], T.slot[:], e_slot)
        load(A, T.sl[16 * k + 64:16 * k + 80, :], T.slot[:], e_slot)
    load(SY, T.xs[:], T.x[:], e_x)

    v_ol = done(V.memset(T.ol[:], 0))
    v_half = done(V.memset(T.half[:], 0.5))
    v_pad = {k: done(V.memset(T["t" + k][:, 4 * CAPP:512], 0.0)) for k in ("next", "prev", "opp", "self")}
    v_mpad = [done(V.memset(T["mt%d" % i][:, 4 * CAPP:512], 0.0)) for i in range(4)]
    z = [done(V.memset(T.et[:, 512 * b:512 * b + 512], 0.0)) for b in (0, 1)]
    wait("A", v_ol)
    load(A, T.ol[0:1, :], T.own[:], e_own)
    load(A, T.ws[:], T.w[:], e_w)
    wait("g", v_half)
    g_id = done(g.affine_select(T.ident[:], T.half[:, 0:128], [[-1, 128]], AluOpType.is_equal, 0.0, 0, 1))
    wait("A", v_half)
    a_flat = done(A.activation(T.flat[:], T.half[:, 0:SLOTS], COPY, scale=0.0))
    z += [done(A.activation(T.et[:, 512 * b:512 * b + 512], T.half[:], COPY, scale=0.0)) for b in (2, 3)]
    wait("A", g_id)
    a_e = []
    for b in range(4):
        wait("A", z[b])
        a_e.append(done(A.activation(T.et[:, 512 * b + b:512 * b + 512:4], T.ident[:], COPY)))

    wait("V", e_want)
    v_w16 = done(V.tensor_scalar(T.w16[:], T.wl[:], 0, 4, AluOpType.max, mult))
    wait("g", v_w16)

    def wcols(k):
        return T.w16[:, 6 * k:6 * k + 6]

    send_two([(nxt, T.lprev[:], wcols(nxt), "l_prev"), (prv, T.lnext[:], wcols(prv), "l_next")])
    send(opp, T.lopp[:], wcols(opp), "l_opp")

    wait("V", e_slot)
    v1 = done(V.tensor_scalar(T.u1[:], T.sl[:], 4, None, AluOpType.arith_shift_right))
    v2 = done(V.tensor_scalar(T.u2[:], T.sl[:], 24, None, mult))
    v_p16 = done(V.tensor_copy(T.pos16[:], T.sl[:]))
    wait("V", v1)
    v3 = done(V.tensor_scalar(T.u3[:], T.u1[:], 1 - SLOTS, None, mult))
    wait("g", v_p16)
    send_two([(nxt, T.pprev[:], T.pos16[:], "p_prev"), (prv, T.pnext[:], T.pos16[:], "p_next")])
    wait("V", v2, v3)
    v_s = [done(V.tensor_tensor(T.so[:, 16 * j:16 * j + 16], T.u2[:], T.u3[:], add)) for j in range(2)]
    wait("V", *v_s)
    v_t = done(V.transpose(T.sot[:], T.so[:]))
    wait("V", v_t)
    v_o = done(V.tensor_copy(T.so16[:], T.sot[:, 0:16]))
    wait("V", e_own, a_flat, v_o)
    v_sc = done(V.tensor_copy(T.flat[:].indirect(T.so16[:]), T.ol[:]))
    wait("SY", v_sc)
    for k in range(8):
        load(SY, T.ownf[16 * k:16 * k + 16, :], T.flat[0:1, :], e_of)

    def xwin(t):
        return T.xs[:, t:4 * R]

    def gather(tile, off):
        ev = []
        for t in range(4):
            out, src = tile[:, t:4 * CAPP:4], xwin(t).indirect(off)
            ev.append(done(V.tensor_copy(out, src)) if t < 2 else done(A.activation(out, src, COPY)))
        return ev

    wait("V", *a_e)
    v_qe = done(V.quantize_mx(T.ec[:], T.ep[:], T.et[:]))
    for q in ("V", "A"):
        wait(q, e_x, v_w16)
    ev = gather(T.tself, wcols(r))
    wait("V", v_pad["self"], *ev)
    v_qs = done(V.quantize_mx(T.lc[:, L_SELF:L_SELF + 128], T.lp[:, L_SELF:L_SELF + 128], T.tself[:]))
    for k, name, back, at, n in ((nxt, "next", "f_prev", L_PREV, nh), (prv, "prev", "f_next", L_NEXT, nh),
                                 (opp, "opp", "f_opp", L_OPP, ne)):
        for q in ("V", "A"):
            wait(q, ("l_" + name, n))
        ev = gather(T["t" + name], T["l" + name][:])
        wait("V", v_pad[name], *ev)
        e = done(V.quantize_mx(T["c" + name][:], T["s" + name][:], T["t" + name][:]))
        wait("g", e)
        send(k, u8(T.lc[:, at:at + CAPP]), u8(T["c" + name][:, 0:CAPP]), back)
        send(k, T.lp[:, at:at + CAPP], T["s" + name][:, 0:CAPP], back)

    wait("V", e_of)
    v_own = done(V.tensor_scalar(T.own16[:], T.ownf[:], 4, None, mult))
    for q in ("V", "A"):
        wait(q, v_own)

    def own_columns(h, t, q):
        out, src = T["xh%d" % h][:, 2 * CAPP * t:2 * CAPP * t + 2 * CAPP], xwin(t).indirect(T.own16[:, 12 * h:12 * h + 12])
        return done(V.tensor_scalar(out, src, 0.5, None, mult) if q == "V" else A.activation(out, src, COPY, scale=0.5))

    ev_x = {r // 2: [own_columns(r // 2, t, "VVAA"[t]) for t in range(4)],
            1 - r // 2: [own_columns(1 - r // 2, t, "A") for t in range(3)]}

    v_m, v_q = {}, {}
    for i, (q, at, skip, arr) in enumerate(((r, L_SELF, 0, v_qs), (prv, L_PREV, 0, ("f_prev", 2 * ne)),
                                            (nxt, L_NEXT - PAD, PAD, ("f_next", 2 * ne)),
                                            (opp, L_OPP, 0, ("f_opp", 2 * ne)))):
        bank, h, c = 4 * (i % 2), q // 2, CAPP * (q % 2)
        m0 = CAPP * i
        wait("PE", v_qe, arr)
        dec, v_m[i] = [], []
        for b in range(4):
            if i > 1:
                wait("PE", v_m[i - 2][b])
            dec.append(done(PE.matmul_mx(T["ps%d" % (bank + b)][:, 0:128], T.ec[:, 128 * b:128 * b + 128], T.ep[:, 128 * b:128 * b + 128],
                                         T.lc[:, at:at + 128], T.lp[:, at:at + 128], True, True)))
        for b in range(4):
            wait("V", dec[b], ev_x[h][b])
            v_m[i].append(done(V.tensor_tensor(T["mt%d" % i][:, b:4 * CAPP:4], T["ps%d" % (bank + b)][:, skip:skip + CAPP],
                                               T["xh%d" % h][:, 2 * CAPP * b + c:2 * CAPP * b + c + CAPP], add)))
        wait("V", v_mpad[i], *v_m[i])
        if i:
            wait("V", v_q[i - 1])
        v_q[i] = done(V.quantize_mx(T.mc[:, m0:m0 + 128], T.mp[:, m0:m0 + 128], T["mt%d" % i][:]))
        wait("g", v_q[i])
        two = [(k, u8(land[:, m0:m0 + CAPP]), u8(T.mc[:, m0:m0 + CAPP]), "m_%s%d" % (name, i))
               for k, land, name in ((nxt, T.prevc, "prev"), (prv, T.nextc, "next"))]
        if i < 3:
            send_two(two)
        else:
            send_two([(nxt, T.prevp[:], T.mp[:, 0:SLOTS], "m_prevp"), (prv, T.nextp[:], T.mp[:, 0:SLOTS], "m_nextp")])
            for w in two:
                send(*w)
        if i == 0:
            ev_x[1 - r // 2].append(own_columns(1 - r // 2, 3, "V"))
    wait("V", e_w)
    v_qw = done(V.quantize_mx(T.wc[:], T.wp[:], T.ws[:]))

    def product(bank, codes, plane, a, n):
        return done(PE.matmul_mx(T["ps%d" % bank][:, 0:n], T.wc[:], T.wp[:], codes[:, a:a + n], plane[:, a:a + n], True, True))

    def copy(q, out, src):
        return done(V.tensor_copy(out, src) if q == "V" else A.activation(out, src, COPY))

    def unload(q, win, s, bank, first, blocks):
        order = (s, (s - 1) % N, (s + 1) % N, (s + 2) % N)
        return [copy(q, win[:, CAPP * order[j]:CAPP * order[j] + CAPP], T["ps%d" % bank][:, CAPP * j - first:CAPP * j - first + CAPP])
                for j in blocks]

    def gather_out(q, out, win, off, j, n):
        return copy(q, out[:, j:j + n], win[:].indirect(off[:, j // 16:(j + n) // 16]))

    wait("PE", v_qw, *[e for i in v_m for e in v_m[i]], *[v_q[i] for i in v_q])
    p = product(0, T.mc, T.mp, 0, SLOTS)
    wait("A", p)
    a_own = unload("A", T.yw1, r, 0, 0, range(4))
    wait("A", v_p16, *a_own)
    a_y1 = gather_out("A", T.ys1, T.yw1, T.pos16, 0, S)
    wait("SY", a_y1)
    load(SY, T.y[:, S:2 * S], T.ys1[:], e_y)
    sides = (("prev", prv, T.prevc, T.prevp, T.yw0), ("next", nxt, T.nextc, T.nextp, T.yw2))
    copies = {}
    for j, (name, s, c, pl, win) in enumerate(sides):
        wait("PE", *[("m_%s%s" % (name, e), nh) for e in "012p"])
        p = product(1 + j, c, pl, 0, 3 * CAPP)
        wait("VA"[j], p)
        copies[name] = unload("VA"[j], win, s, 1 + j, 0, range(3))
    for j, (name, s, c, pl, win) in enumerate(sides):
        wait("PE", ("m_%s3" % name, ne))
        p = product(3 + j, c, pl, SLOTS - 128, 128)
        wait("V", p)
        copies[name] += unload("V", win, s, 3 + j, SLOTS - 128, (3,))
        out, off, at = (T.ys0, T.pprev, 0) if j == 0 else (T.ys2, T.pnext, 2 * S)
        for q, a, sq in (("V", 0, "SY"), ("A", 128, "A" if j else "SY")):
            wait(q, ("p_" + name, nh), *copies[name])
            e = gather_out(q, out, win, off, a, 128)
            wait(sq, e)
            load(queues[sq], T.y[:, at + a:at + a + 128], out[:, a:a + 128], e_y)

    wait("g", e_y, ("sent", sent[0]))
    wait("g", *list(unwaited.items()))
